import numpy as np
import ml_dtypes

BF16 = ml_dtypes.bfloat16


def bf(x):
    return np.asarray(x, np.float32).astype(BF16)


def f32(x):
    return np.asarray(x, np.float32)


def f64(x):
    return np.asarray(x).astype(np.float64)


def striped(idx):
    return np.tile(idx.reshape(-1, 16).T, (8, 1))


S, K, M, N, E, Q = 512, 128, 256, 1024, 8, 128


def two_experts():
    first = np.random.permutation(S).reshape(E, S // E)
    return np.concatenate([np.random.permutation(np.concatenate([first[e], first[(e + 1) % E]])) for e in range(E)])


def setup_inputs():
    return {"table": bf(np.random.standard_normal((S, K))), "w": bf(np.random.standard_normal((E, K, M)) / np.sqrt(K)), "b": f32(0.5 * np.random.standard_normal((M, 1))), "offs": striped(two_experts())}


def reference(table, w, b, offs):
    idx = offs[:16].T.reshape(-1)
    x = f64(table)[idx].T
    y = np.concatenate([f64(w)[e].T @ x[:, e * Q : (e + 1) * Q] for e in range(E)], axis=1)
    return np.maximum(y + f64(b), 0.0)

@@ -1,0 +1,59 @@
+import concourse.mybir as mybir
+from concourse.masks import make_identity
+
+BF16, F32, U16 = mybir.dt.bfloat16, mybir.dt.float32, mybir.dt.uint16
+ADD, MAX = mybir.AluOpType.add, mybir.AluOpType.max
+RELU = mybir.ActivationFunctionType.Relu
+
+P = 128
+S, K, M, N, E, Q = 512, 128, 256, 1024, 8, 128
+BANK = 512
+FLOPS = 2 * K * M * N
+
+
+def tile_gather_matmul_kernel(tc, table, w, b, offs, out):
+    nc = tc.nc
+    with (
+        tc.tile_pool(name="held", bufs=1) as held,
+        tc.psum_pool(name="psum", bufs=1) as psum,
+    ):
+        offsets = held.tile([P, N // 16], U16, name="offsets")
+        nc.sync.dma_start(offsets[:], offs)
+        rows = held.tile([P, S // P, K], BF16, name="rows")
+        nc.sync.dma_start(rows[:], table.rearrange("(t p) k -> p t k", p=P))
+        weights = held.tile([P, E, M], BF16, name="weights")
+        nc.scalar.dma_start(weights[:], w.rearrange("e k m -> k e m"))
+        identity = held.tile([P, P], BF16, name="identity")
+        make_identity(nc, identity[:])
+        bias = held.tile([P, M // P], F32, name="bias")
+        with nc.allow_non_contiguous_dma(reason="one float32 to a partition"):
+            nc.gpsimd.dma_start(bias[:], b.rearrange("(a p) o -> p (a o)", p=P))
+
+        flipped = psum.tile([P, S], BF16, name="flipped")
+        for t in range(S // P):
+            nc.tensor.transpose(flipped[:, t * P : (t + 1) * P], rows[:, t, :], identity[:])
+        tokens = held.tile([P, S], BF16, name="tokens")
+        nc.vector.tensor_copy(tokens[:], flipped[:])
+
+        banks = [
+            [psum.tile([P, BANK], F32, name=f"bank{a}{h}") for h in range(N // BANK)]
+            for a in range(M // P)
+        ]
+        staged = [held.tile([P, N], F32, name=f"staged{a}") for a in range(M // P)]
+        for h in range(N // BANK):
+            for e in range(h * BANK // Q, (h + 1) * BANK // Q):
+                picked = tokens[:].indirect(offsets[:, e * Q // 16 : (e + 1) * Q // 16])
+                column = e * Q - h * BANK
+                for a in range(M // P):
+                    nc.tensor.matmul(
+                        banks[a][h][:, column : column + Q],
+                        weights[:, e, a * P : (a + 1) * P],
+                        picked,
+                        start=True,
+                        stop=True,
+                    )
+            part = slice(h * BANK, (h + 1) * BANK)
+            nc.scalar.activation(staged[0][:, part], banks[0][h][:], RELU, bias=bias[:, 0:1])
+            nc.vector.tensor_scalar(staged[1][:, part], banks[1][h][:], bias[:, 1:2], 0.0, op0=ADD, op1=MAX)
+            nc.sync.dma_start(out[0:P, part], staged[0][:, part])
+            nc.scalar.dma_start(out[P : 2 * P, part], staged[1][:, part])

@@ -7,53 +7,61 @@ RELU = mybir.ActivationFunctionType.Relu
 
 P = 128
 S, K, M, N, E, Q = 512, 128, 256, 1024, 8, 128
-BANK = 512
 FLOPS = 2 * K * M * N
+PAIR = 2 * Q
+BANK = 512
+WARM = 4
 
 
 def tile_gather_matmul_kernel(tc, table, w, b, offs, out):
     nc = tc.nc
     with (
         tc.tile_pool(name="held", bufs=1) as held,
-        tc.psum_pool(name="psum", bufs=1) as psum,
+        tc.tile_pool(name="work", bufs=N // PAIR * M // P) as work,
+        tc.psum_pool(name="flip", bufs=1) as flip,
+        tc.psum_pool(name="psum", bufs=6) as psum,
     ):
+        zeros = held.tile([P, BANK], BF16, name="zeros")
+        nc.vector.memset(zeros[:], 0.0)
+        unused = flip.tile([P, BANK], F32, name="unused")
+        for turn in range(WARM):
+            nc.tensor.matmul(unused[:], zeros[:, 0:P], zeros[:], start=True, stop=True)
+
         offsets = held.tile([P, N // 16], U16, name="offsets")
         nc.sync.dma_start(offsets[:], offs)
         rows = held.tile([P, S // P, K], BF16, name="rows")
-        nc.sync.dma_start(rows[:], table.rearrange("(t p) k -> p t k", p=P))
+        nc.scalar.dma_start(rows[:], table.rearrange("(t p) k -> p t k", p=P))
         weights = held.tile([P, E, M], BF16, name="weights")
-        nc.scalar.dma_start(weights[:], w.rearrange("e k m -> k e m"))
-        identity = held.tile([P, P], BF16, name="identity")
-        make_identity(nc, identity[:])
+        nc.sync.dma_start(weights[:], w.rearrange("e k m -> k e m"))
         bias = held.tile([P, M // P], F32, name="bias")
         with nc.allow_non_contiguous_dma(reason="one float32 to a partition"):
-            nc.gpsimd.dma_start(bias[:], b.rearrange("(a p) o -> p (a o)", p=P))
+            nc.scalar.dma_start(bias[:], b.rearrange("(a p) o -> p (a o)", p=P))
+        identity = held.tile([P, P], BF16, name="identity")
+        make_identity(nc, identity[:])
 
-        flipped = psum.tile([P, S], BF16, name="flipped")
+        flipped = flip.tile([P, S], BF16, name="flipped")
         for t in range(S // P):
             nc.tensor.transpose(flipped[:, t * P : (t + 1) * P], rows[:, t, :], identity[:])
         tokens = held.tile([P, S], BF16, name="tokens")
         nc.vector.tensor_copy(tokens[:], flipped[:])
 
-        banks = [
-            [psum.tile([P, BANK], F32, name=f"bank{a}{h}") for h in range(N // BANK)]
-            for a in range(M // P)
-        ]
-        staged = [held.tile([P, N], F32, name=f"staged{a}") for a in range(M // P)]
-        for h in range(N // BANK):
-            for e in range(h * BANK // Q, (h + 1) * BANK // Q):
-                picked = tokens[:].indirect(offsets[:, e * Q // 16 : (e + 1) * Q // 16])
-                column = e * Q - h * BANK
-                for a in range(M // P):
+        for g in range(N // PAIR):
+            for a in range(M // P):
+                product = psum.tile([P, PAIR], F32, name="product")
+                for i in range(PAIR // Q):
+                    e = g * (PAIR // Q) + i
                     nc.tensor.matmul(
-                        banks[a][h][:, column : column + Q],
+                        product[:, i * Q : (i + 1) * Q],
                         weights[:, e, a * P : (a + 1) * P],
-                        picked,
+                        tokens[:].indirect(offsets[:, e * Q // 16 : (e + 1) * Q // 16]),
                         start=True,
                         stop=True,
                     )
-            part = slice(h * BANK, (h + 1) * BANK)
-            nc.scalar.activation(staged[0][:, part], banks[0][h][:], RELU, bias=bias[:, 0:1])
-            nc.vector.tensor_scalar(staged[1][:, part], banks[1][h][:], bias[:, 1:2], 0.0, op0=ADD, op1=MAX)
-            nc.sync.dma_start(out[0:P, part], staged[0][:, part])
-            nc.scalar.dma_start(out[P : 2 * P, part], staged[1][:, part])
+                staged = work.tile([P, PAIR], F32, name="staged")
+                target = out[a * P : (a + 1) * P, g * PAIR : (g + 1) * PAIR]
+                if a == 0:
+                    nc.scalar.activation(staged[:], product[:], RELU, bias=bias[:, a : a + 1])
+                    nc.scalar.dma_start(target, staged[:])
+                else:
+                    nc.vector.tensor_scalar(staged[:], product[:], bias[:, a : a + 1], 0.0, op0=ADD, op1=MAX)
+                    nc.sync.dma_start(target, staged[:])

@@ -7,58 +7,63 @@ RELU = mybir.ActivationFunctionType.Relu
 
 P = 128
 S, K, M, N, E, Q = 512, 128, 256, 1024, 8, 128
-FLOPS = 2 * K * M * N
-PAIR = 2 * Q
-BANK = 512
+TOKEN_BLOCKS = S // P
+OUT_BLOCKS = M // P
+DUO = 2
+BANKS, BANK = 8, 512
 WARM = 4
+FLOPS = 2 * K * M * N
 
 
 def tile_gather_matmul_kernel(tc, table, w, b, offs, out):
     nc = tc.nc
     with (
         tc.tile_pool(name="held", bufs=1) as held,
-        tc.tile_pool(name="work", bufs=N // PAIR * M // P) as work,
-        tc.psum_pool(name="flip", bufs=1) as flip,
-        tc.psum_pool(name="psum", bufs=6) as psum,
+        tc.tile_pool(name="work", bufs=E // DUO * OUT_BLOCKS) as work,
+        tc.psum_pool(name="once", bufs=1) as once,
+        tc.psum_pool(name="psum", bufs=BANKS - 2) as psum,
     ):
-        zeros = held.tile([P, BANK], BF16, name="zeros")
-        nc.vector.memset(zeros[:], 0.0)
-        unused = flip.tile([P, BANK], F32, name="unused")
-        for turn in range(WARM):
-            nc.tensor.matmul(unused[:], zeros[:, 0:P], zeros[:], start=True, stop=True)
-
         offsets = held.tile([P, N // 16], U16, name="offsets")
         nc.sync.dma_start(offsets[:], offs)
-        rows = held.tile([P, S // P, K], BF16, name="rows")
+        rows = held.tile([P, TOKEN_BLOCKS, K], BF16, name="rows")
         nc.scalar.dma_start(rows[:], table.rearrange("(t p) k -> p t k", p=P))
-        weights = held.tile([P, E, M], BF16, name="weights")
-        nc.sync.dma_start(weights[:], w.rearrange("e k m -> k e m"))
-        bias = held.tile([P, M // P], F32, name="bias")
+        weights = [held.tile([P, DUO, M], BF16, name=f"weights{g}") for g in range(E // DUO)]
+        for g in range(E // DUO):
+            nc.sync.dma_start(weights[g][:], w[g * DUO : (g + 1) * DUO].rearrange("e k m -> k e m"))
+        bias = held.tile([P, OUT_BLOCKS], F32, name="bias")
         with nc.allow_non_contiguous_dma(reason="one float32 to a partition"):
             nc.scalar.dma_start(bias[:], b.rearrange("(a p) o -> p (a o)", p=P))
         identity = held.tile([P, P], BF16, name="identity")
         make_identity(nc, identity[:])
 
-        flipped = flip.tile([P, S], BF16, name="flipped")
-        for t in range(S // P):
+        zeros = held.tile([P, BANK], BF16, name="zeros")
+        nc.vector.memset(zeros[:], 0.0)
+        unused = once.tile([P, BANK], F32, name="unused")
+        for turn in range(WARM):
+            nc.tensor.matmul(unused[:], zeros[:, 0:P], zeros[:], start=True, stop=True)
+        primed = held.tile([P, 1], F32, name="primed")
+        nc.scalar.activation(primed[:], zeros[:, 0:1], RELU)
+
+        flipped = once.tile([P, S], BF16, name="flipped")
+        for t in range(TOKEN_BLOCKS):
             nc.tensor.transpose(flipped[:, t * P : (t + 1) * P], rows[:, t, :], identity[:])
         tokens = held.tile([P, S], BF16, name="tokens")
         nc.vector.tensor_copy(tokens[:], flipped[:])
 
-        for g in range(N // PAIR):
-            for a in range(M // P):
-                product = psum.tile([P, PAIR], F32, name="product")
-                for i in range(PAIR // Q):
-                    e = g * (PAIR // Q) + i
+        for g in range(E // DUO):
+            for a in range(OUT_BLOCKS):
+                product = psum.tile([P, DUO * Q], F32, name="product")
+                for i in range(DUO):
+                    e = g * DUO + i
                     nc.tensor.matmul(
                         product[:, i * Q : (i + 1) * Q],
-                        weights[:, e, a * P : (a + 1) * P],
+                        weights[g][:, i, a * P : (a + 1) * P],
                         tokens[:].indirect(offsets[:, e * Q // 16 : (e + 1) * Q // 16]),
                         start=True,
                         stop=True,
                     )
-                staged = work.tile([P, PAIR], F32, name="staged")
-                target = out[a * P : (a + 1) * P, g * PAIR : (g + 1) * PAIR]
+                staged = work.tile([P, DUO * Q], F32, name="staged")
+                target = out[a * P : (a + 1) * P, g * DUO * Q : (g + 1) * DUO * Q]
                 if a == 0:
                     nc.scalar.activation(staged[:], product[:], RELU, bias=bias[:, a : a + 1])
                     nc.scalar.dma_start(target, staged[:])

@@ -10,8 +10,7 @@ S, K, M, N, E, Q = 512, 128, 256, 1024, 8, 128
 TOKEN_BLOCKS = S // P
 OUT_BLOCKS = M // P
 DUO = 2
-BANKS, BANK = 8, 512
-WARM = 4
+BANKS = 8
 FLOPS = 2 * K * M * N
 
 
@@ -21,7 +20,7 @@ def tile_gather_matmul_kernel(tc, table, w, b, offs, out):
         tc.tile_pool(name="held", bufs=1) as held,
         tc.tile_pool(name="work", bufs=E // DUO * OUT_BLOCKS) as work,
         tc.psum_pool(name="once", bufs=1) as once,
-        tc.psum_pool(name="psum", bufs=BANKS - 2) as psum,
+        tc.psum_pool(name="psum", bufs=BANKS - 1) as psum,
     ):
         offsets = held.tile([P, N // 16], U16, name="offsets")
         nc.sync.dma_start(offsets[:], offs)
@@ -36,13 +35,10 @@ def tile_gather_matmul_kernel(tc, table, w, b, offs, out):
         identity = held.tile([P, P], BF16, name="identity")
         make_identity(nc, identity[:])
 
-        zeros = held.tile([P, BANK], BF16, name="zeros")
+        zeros = held.tile([P, 1], F32, name="zeros")
         nc.vector.memset(zeros[:], 0.0)
-        unused = once.tile([P, BANK], F32, name="unused")
-        for turn in range(WARM):
-            nc.tensor.matmul(unused[:], zeros[:, 0:P], zeros[:], start=True, stop=True)
         primed = held.tile([P, 1], F32, name="primed")
-        nc.scalar.activation(primed[:], zeros[:, 0:1], RELU)
+        nc.scalar.activation(primed[:], zeros[:], RELU)
 
         flipped = once.tile([P, S], BF16, name="flipped")
         for t in range(TOKEN_BLOCKS):

@@ -62,7 +62,6 @@ def tile_gather_matmul_kernel(tc, table, w, b, offs, out):
                 target = out[a * P : (a + 1) * P, g * DUO * Q : (g + 1) * DUO * Q]
                 if a == 0:
                     nc.scalar.activation(staged[:], product[:], RELU, bias=bias[:, a : a + 1])
-                    nc.scalar.dma_start(target, staged[:])
                 else:
                     nc.vector.tensor_scalar(staged[:], product[:], bias[:, a : a + 1], 0.0, op0=ADD, op1=MAX)
-                    nc.sync.dma_start(target, staged[:])
+                nc.sync.dma_start(target, staged[:])

@@ -19,8 +19,8 @@ def tile_gather_matmul_kernel(tc, table, w, b, offs, out):
     with (
         tc.tile_pool(name="held", bufs=1) as held,
         tc.tile_pool(name="work", bufs=E // DUO * OUT_BLOCKS) as work,
-        tc.psum_pool(name="once", bufs=1) as once,
-        tc.psum_pool(name="psum", bufs=BANKS - 1) as psum,
+        tc.psum_pool(name="once", bufs=TOKEN_BLOCKS) as once,
+        tc.psum_pool(name="psum", bufs=BANKS - TOKEN_BLOCKS) as psum,
     ):
         offsets = held.tile([P, N // 16], U16, name="offsets")
         nc.sync.dma_start(offsets[:], offs)
@@ -40,11 +40,11 @@ def tile_gather_matmul_kernel(tc, table, w, b, offs, out):
         primed = held.tile([P, 1], F32, name="primed")
         nc.scalar.activation(primed[:], zeros[:], RELU)
 
-        flipped = once.tile([P, S], BF16, name="flipped")
-        for t in range(TOKEN_BLOCKS):
-            nc.tensor.transpose(flipped[:, t * P : (t + 1) * P], rows[:, t, :], identity[:])
         tokens = held.tile([P, S], BF16, name="tokens")
-        nc.vector.tensor_copy(tokens[:], flipped[:])
+        for t in range(TOKEN_BLOCKS):
+            flipped = once.tile([P, P], BF16, name="flipped")
+            nc.tensor.transpose(flipped[:], rows[:, t, :], identity[:])
+            nc.vector.tensor_copy(tokens[:, t * P : (t + 1) * P], flipped[:])
 
         for g in range(E // DUO):
             for a in range(OUT_BLOCKS):

@@ -3,7 +3,6 @@ from concourse.masks import make_identity
 
 BF16, F32, U16 = mybir.dt.bfloat16, mybir.dt.float32, mybir.dt.uint16
 ADD, MAX = mybir.AluOpType.add, mybir.AluOpType.max
-RELU = mybir.ActivationFunctionType.Relu
 
 P = 128
 S, K, M, N, E, Q = 512, 128, 256, 1024, 8, 128
@@ -35,11 +34,6 @@ def tile_gather_matmul_kernel(tc, table, w, b, offs, out):
         identity = held.tile([P, P], BF16, name="identity")
         make_identity(nc, identity[:])
 
-        zeros = held.tile([P, 1], F32, name="zeros")
-        nc.vector.memset(zeros[:], 0.0)
-        primed = held.tile([P, 1], F32, name="primed")
-        nc.scalar.activation(primed[:], zeros[:], RELU)
-
         tokens = held.tile([P, S], BF16, name="tokens")
         for t in range(TOKEN_BLOCKS):
             flipped = once.tile([P, P], BF16, name="flipped")
@@ -60,8 +54,5 @@ def tile_gather_matmul_kernel(tc, table, w, b, offs, out):
                     )
                 staged = work.tile([P, DUO * Q], F32, name="staged")
                 target = out[a * P : (a + 1) * P, g * DUO * Q : (g + 1) * DUO * Q]
-                if a == 0:
-                    nc.scalar.activation(staged[:], product[:], RELU, bias=bias[:, a : a + 1])
-                else:
-                    nc.vector.tensor_scalar(staged[:], product[:], bias[:, a : a + 1], 0.0, op0=ADD, op1=MAX)
+                nc.vector.tensor_scalar(staged[:], product[:], bias[:, a : a + 1], 0.0, op0=ADD, op1=MAX)
                 nc.sync.dma_start(target, staged[:])

@@ -18,8 +18,7 @@ def tile_gather_matmul_kernel(tc, table, w, b, offs, out):
     with (
         tc.tile_pool(name="held", bufs=1) as held,
         tc.tile_pool(name="work", bufs=E // DUO * OUT_BLOCKS) as work,
-        tc.psum_pool(name="once", bufs=TOKEN_BLOCKS) as once,
-        tc.psum_pool(name="psum", bufs=BANKS - TOKEN_BLOCKS) as psum,
+        tc.psum_pool(name="psum", bufs=BANKS) as psum,
     ):
         offsets = held.tile([P, N // 16], U16, name="offsets")
         nc.sync.dma_start(offsets[:], offs)
@@ -36,23 +35,24 @@ def tile_gather_matmul_kernel(tc, table, w, b, offs, out):
 
         tokens = held.tile([P, S], BF16, name="tokens")
         for t in range(TOKEN_BLOCKS):
-            flipped = once.tile([P, P], BF16, name="flipped")
+            flipped = psum.tile([P, P], BF16, name="flipped", tag="bank")
             nc.tensor.transpose(flipped[:], rows[:, t, :], identity[:])
             nc.vector.tensor_copy(tokens[:, t * P : (t + 1) * P], flipped[:])
 
         for g in range(E // DUO):
             for a in range(OUT_BLOCKS):
-                product = psum.tile([P, DUO * Q], F32, name="product")
+                staged = work.tile([P, DUO * Q], F32, name="staged")
                 for i in range(DUO):
                     e = g * DUO + i
+                    product = psum.tile([P, Q], F32, name="product", tag="bank")
                     nc.tensor.matmul(
-                        product[:, i * Q : (i + 1) * Q],
+                        product[:],
                         weights[g][:, i, a * P : (a + 1) * P],
                         tokens[:].indirect(offsets[:, e * Q // 16 : (e + 1) * Q // 16]),
                         start=True,
                         stop=True,
                     )
-                staged = work.tile([P, DUO * Q], F32, name="staged")
-                target = out[a * P : (a + 1) * P, g * DUO * Q : (g + 1) * DUO * Q]
-                nc.vector.tensor_scalar(staged[:], product[:], bias[:, a : a + 1], 0.0, op0=ADD, op1=MAX)
-                nc.sync.dma_start(target, staged[:])
+                    nc.vector.tensor_scalar(
+                        staged[:, i * Q : (i + 1) * Q], product[:], bias[:, a : a + 1], 0.0, op0=ADD, op1=MAX
+                    )
+                nc.sync.dma_start(out[a * P : (a + 1) * P, g * DUO * Q : (g + 1) * DUO * Q], staged[:])

@@ -8,6 +8,7 @@ P = 128
 S, K, M, N, E, Q = 512, 128, 256, 1024, 8, 128
 TOKEN_BLOCKS = S // P
 OUT_BLOCKS = M // P
+WARM_TURNS = 4
 DUO = 2
 BANKS = 8
 FLOPS = 2 * K * M * N
@@ -18,7 +19,8 @@ def tile_gather_matmul_kernel(tc, table, w, b, offs, out):
     with (
         tc.tile_pool(name="held", bufs=1) as held,
         tc.tile_pool(name="work", bufs=E // DUO * OUT_BLOCKS) as work,
-        tc.psum_pool(name="psum", bufs=BANKS) as psum,
+        tc.psum_pool(name="psum", bufs=BANKS - 1) as psum,
+        tc.psum_pool(name="unread", bufs=1) as unread,
     ):
         offsets = held.tile([P, N // 16], U16, name="offsets")
         nc.sync.dma_start(offsets[:], offs)
@@ -32,6 +34,12 @@ def tile_gather_matmul_kernel(tc, table, w, b, offs, out):
             nc.scalar.dma_start(bias[:], b.rearrange("(a p) o -> p (a o)", p=P))
         identity = held.tile([P, P], BF16, name="identity")
         make_identity(nc, identity[:])
+
+        zeros = held.tile([P, P], BF16, name="zeros")
+        nc.vector.memset(zeros[:], 0.0)
+        warm = unread.tile([P, 4, P], F32, name="warm")
+        for turn in range(WARM_TURNS):
+            nc.tensor.matmul(warm[:], zeros[:], zeros[:].unsqueeze(1).to_broadcast([P, 4, P]), start=True, stop=True)
 
         tokens = held.tile([P, S], BF16, name="tokens")
         for t in range(TOKEN_BLOCKS):

@@ -8,7 +8,7 @@ P = 128
 S, K, M, N, E, Q = 512, 128, 256, 1024, 8, 128
 TOKEN_BLOCKS = S // P
 OUT_BLOCKS = M // P
-WARM_TURNS = 4
+WARM_TURNS = 3
 DUO = 2
 BANKS = 8
 FLOPS = 2 * K * M * N

@@ -60,7 +60,11 @@ def tile_gather_matmul_kernel(tc, table, w, b, offs, out):
                         start=True,
                         stop=True,
                     )
+                    columns = slice(i * Q, (i + 1) * Q)
                     nc.vector.tensor_scalar(
-                        staged[:, i * Q : (i + 1) * Q], product[:], bias[:, a : a + 1], 0.0, op0=ADD, op1=MAX
+                        staged[:, columns], product[:], bias[:, a : a + 1], 0.0, op0=ADD, op1=MAX
                     )
-                nc.sync.dma_start(out[a * P : (a + 1) * P, g * DUO * Q : (g + 1) * DUO * Q], staged[:])
+                    if (g, a) == (0, 0):
+                        nc.sync.dma_start(out[:P, columns], staged[:, columns])
+                if (g, a) != (0, 0):
+                    nc.sync.dma_start(out[a * P : (a + 1) * P, g * DUO * Q : (g + 1) * DUO * Q], staged[:])

@@ -22,16 +22,17 @@ def tile_gather_matmul_kernel(tc, table, w, b, offs, out):
         tc.psum_pool(name="psum", bufs=BANKS - 1) as psum,
         tc.psum_pool(name="unread", bufs=1) as unread,
     ):
+        rows = held.tile([P, TOKEN_BLOCKS, K], BF16, name="rows")
+        nc.sync.dma_start(rows[:], table.rearrange("(t p) k -> p t k", p=P))
         offsets = held.tile([P, N // 16], U16, name="offsets")
         nc.sync.dma_start(offsets[:], offs)
-        rows = held.tile([P, TOKEN_BLOCKS, K], BF16, name="rows")
-        nc.scalar.dma_start(rows[:], table.rearrange("(t p) k -> p t k", p=P))
         weights = [held.tile([P, DUO, M], BF16, name=f"weights{g}") for g in range(E // DUO)]
         for g in range(E // DUO):
             nc.sync.dma_start(weights[g][:], w[g * DUO : (g + 1) * DUO].rearrange("e k m -> k e m"))
-        bias = held.tile([P, OUT_BLOCKS], F32, name="bias")
-        with nc.allow_non_contiguous_dma(reason="one float32 to a partition"):
-            nc.scalar.dma_start(bias[:], b.rearrange("(a p) o -> p (a o)", p=P))
+            if g == 0:
+                bias = held.tile([P, OUT_BLOCKS], F32, name="bias")
+                with nc.allow_non_contiguous_dma(reason="one float32 to a partition"):
+                    nc.sync.dma_start(bias[:], b.rearrange("(a p) o -> p (a o)", p=P))
         identity = held.tile([P, P], BF16, name="identity")
         make_identity(nc, identity[:])
 

import concourse.mybir as mybir
from concourse.masks import make_identity

BF16, F32, U16 = mybir.dt.bfloat16, mybir.dt.float32, mybir.dt.uint16
ADD, MAX = mybir.AluOpType.add, mybir.AluOpType.max

P = 128
S, K, M, N, E, Q = 512, 128, 256, 1024, 8, 128
TOKEN_BLOCKS = S // P
OUT_BLOCKS = M // P
WARM_TURNS = 3
DUO = 2
BANKS = 8
FLOPS = 2 * K * M * N


def tile_gather_matmul_kernel(tc, table, w, b, offs, out):
    nc = tc.nc
    with (
        tc.tile_pool(name="held", bufs=1) as held,
        tc.tile_pool(name="work", bufs=E // DUO * OUT_BLOCKS) as work,
        tc.psum_pool(name="psum", bufs=BANKS - 1) as psum,
        tc.psum_pool(name="unread", bufs=1) as unread,
    ):
        rows = held.tile([P, TOKEN_BLOCKS, K], BF16, name="rows")
        nc.sync.dma_start(rows[:], table.rearrange("(t p) k -> p t k", p=P))
        offsets = held.tile([P, N // 16], U16, name="offsets")
        nc.sync.dma_start(offsets[:], offs)
        weights = [held.tile([P, DUO, M], BF16, name=f"weights{g}") for g in range(E // DUO)]
        for g in range(E // DUO):
            nc.sync.dma_start(weights[g][:], w[g * DUO : (g + 1) * DUO].rearrange("e k m -> k e m"))
            if g == 0:
                bias = held.tile([P, OUT_BLOCKS], F32, name="bias")
                with nc.allow_non_contiguous_dma(reason="one float32 to a partition"):
                    nc.sync.dma_start(bias[:], b.rearrange("(a p) o -> p (a o)", p=P))
        identity = held.tile([P, P], BF16, name="identity")
        make_identity(nc, identity[:])

        zeros = held.tile([P, P], BF16, name="zeros")
        nc.vector.memset(zeros[:], 0.0)
        warm = unread.tile([P, 4, P], F32, name="warm")
        for turn in range(WARM_TURNS):
            nc.tensor.matmul(warm[:], zeros[:], zeros[:].unsqueeze(1).to_broadcast([P, 4, P]), start=True, stop=True)

        tokens = held.tile([P, S], BF16, name="tokens")
        for t in range(TOKEN_BLOCKS):
            flipped = psum.tile([P, P], BF16, name="flipped", tag="bank")
            nc.tensor.transpose(flipped[:], rows[:, t, :], identity[:])
            nc.vector.tensor_copy(tokens[:, t * P : (t + 1) * P], flipped[:])

        for g in range(E // DUO):
            for a in range(OUT_BLOCKS):
                staged = work.tile([P, DUO * Q], F32, name="staged")
                for i in range(DUO):
                    e = g * DUO + i
                    product = psum.tile([P, Q], F32, name="product", tag="bank")
                    nc.tensor.matmul(
                        product[:],
                        weights[g][:, i, a * P : (a + 1) * P],
                        tokens[:].indirect(offsets[:, e * Q // 16 : (e + 1) * Q // 16]),
                        start=True,
                        stop=True,
                    )
                    columns = slice(i * Q, (i + 1) * Q)
                    nc.vector.tensor_scalar(
                        staged[:, columns], product[:], bias[:, a : a + 1], 0.0, op0=ADD, op1=MAX
                    )
                    if (g, a) == (0, 0):
                        nc.sync.dma_start(out[:P, columns], staged[:, columns])
                if (g, a) != (0, 0):
                    nc.sync.dma_start(out[a * P : (a + 1) * P, g * DUO * Q : (g + 1) * DUO * Q], staged[:])
